import numpy as np
import ml_dtypes


def mxq(x, axis, fmt="e4m3"):
    dtype, down = {"e4m3": (ml_dtypes.float8_e4m3fn, 7), "e5m2": (ml_dtypes.float8_e5m2, 14)}[fmt]
    v = np.moveaxis(np.asarray(x, np.float32).astype(ml_dtypes.bfloat16).astype(np.float64), axis, -1)
    blocks = v.reshape(v.shape[:-1] + (-1, 32))
    amax = np.abs(blocks).max(-1, keepdims=True)
    byte = np.maximum(np.where(amax > 0, np.frexp(amax)[1] - 1 + 127, 0) - down, 1)
    scale = np.exp2(byte - 127.0)
    codes = (blocks / scale).astype(np.float32).astype(dtype).astype(np.float64)
    return np.moveaxis((codes * scale).reshape(v.shape), -1, axis)


WIDE = False


def mx_kscale(k, group=512):
    if not WIDE:
        return np.ones(k)
    levels = np.array([18, -18])
    if group != 512:
        return np.exp2(np.random.permutation(np.resize(levels, k // group))).repeat(group)
    if k % 512:
        return np.exp2(np.random.permutation(np.resize(levels, k // 32))).repeat(32)
    a = np.empty((k // 512, 16))
    for p in range(k // 512):
        a[p, :8] = np.random.permutation(np.resize(levels, 8))
        for g in range(8):
            far = levels[np.abs(levels - a[p, g]) >= 10]
            a[p, g + 8] = far[np.random.randint(len(far))]
    return np.exp2(a.ravel()).repeat(32)


def f64(x):
    return np.asarray(x).astype(np.float64)


G, D, M, N, K, L = 4, 128, 128, 512, 128, 128


def sgn(shape):
    return np.random.uniform(0.5, 2.0, shape) * np.where(np.random.standard_normal(shape) < 0, -1.0, 1.0)


def setup_inputs():
    n = np.random.standard_normal
    s_d = mx_kscale(D, 0)
    s_m = mx_kscale(M, 0)
    s_k = mx_kscale(K, 0)
    return {
        "h": (n((G, D, N)) * s_d[:, None]).astype(np.float32),
        "w1": (n((G, D, M)) / np.sqrt(D) / s_d[:, None]).astype(np.float32),
        "x1": (n((G, M, N))).astype(np.float32),
        "a1": (sgn((G, M, 1)) * s_m[:, None]).astype(np.float32),
        "w2": (n((G, M, K)) / np.sqrt(M) / s_m[:, None]).astype(np.float32),
        "x2": (n((G, K, N))).astype(np.float32),
        "a2": (sgn((G, K, 1)) * s_k[:, None]).astype(np.float32),
        "w3": (n((G, K, L)) / np.sqrt(K) / s_k[:, None]).astype(np.float32),
        "x3": (n((G, L, N))).astype(np.float32),
    }


def reference(h, w1, x1, a1, w2, x2, a2, w3, x3):
    w1q = mxq(f64(w1), 1, "e4m3")
    hq = mxq(f64(h), 1, "e4m3")
    z1 = w1q.transpose(0, 2, 1) @ hq
    h1 = np.maximum(z1 + f64(x1), 0.0) * f64(a1)
    w2q = mxq(f64(w2), 1, "e4m3")
    h1q = mxq(h1, 1, "e4m3")
    z2 = w2q.transpose(0, 2, 1) @ h1q
    h2 = np.maximum(z2 + f64(x2), 0.0) * f64(a2)
    w3q = mxq(f64(w3), 1, "e4m3")
    h2q = mxq(h2, 1, "e4m3")
    z3 = w3q.transpose(0, 2, 1) @ h2q
    y = np.maximum(z3 + f64(x3), 0.0)
    return y

@@ -1,0 +1,259 @@
+from contextlib import ExitStack
+
+import concourse.mybir as mybir
+
+G, D, N = 4, 128, 512
+FLOPS = 3 * 2 * G * D * D * N
+
+F32 = mybir.dt.float32
+BF16 = mybir.dt.bfloat16
+I32 = mybir.dt.int32
+U8 = mybir.dt.uint8
+FP8X4 = mybir.dt.float8_e4m3fn_x4
+ALU = mybir.AluOpType
+ACT = mybir.ActivationFunctionType
+
+P = 128
+R = 32
+PACK = 4
+C = 128
+LEAD = 96
+PLANE = 96
+SLOT = D + PLANE
+H_SPLIT = 176
+HEAD_ORDER = (0, 3, 1, 2)
+QUADRANT_ORDER = (0, 2, 1, 3)
+SLOT_OF_SHIFT = (0, 2, 1, 3)
+
+
+def tile_rows_steps_relu_kernel(tc, h, w1, x1, a1, w2, x2, a2, w3, x3, out):
+    nc = tc.nc
+    with ExitStack() as ctx:
+        sb = ctx.enter_context(tc.tile_pool(name="sb", bufs=1))
+        ps = ctx.enter_context(tc.psum_pool(name="ps", bufs=1))
+        ctx.enter_context(tc.manual_schedule())
+
+        def tile(name, shape, dtype):
+            return sb.tile(shape, dtype, name=name, align_bytes=64)
+
+        bank_a = [ps.tile([P, N], F32, name="bank_a%d" % r) for r in range(G)]
+        bank_b = [ps.tile([P, N], F32, name="bank_b%d" % r) for r in range(G)]
+
+        w1_raw = tile("w1_raw", [P, PACK, D], F32)
+        w2_raw = tile("w2_raw", [P, PACK, D], F32)
+        w3_raw = tile("w3_raw", [P, PACK, D], F32)
+        h_raw = tile("h_raw", [P, PACK, N], F32)
+        x1_raw = tile("x1_raw", [P, G, PACK, C], F32)
+        x2_raw = tile("x2_raw", [P, PACK, N], F32)
+        x3_raw = tile("x3_raw", [P, G, N], F32)
+        a1_head = tile("a1_head", [P, PACK], F32)
+        a2_head = tile("a2_head", [P, PACK], F32)
+        a1_all = tile("a1_all", [P, G, PACK], F32)
+        sign1 = tile("sign1", [P, PACK], F32)
+        sign2 = tile("sign2", [P, PACK], F32)
+        abs1 = tile("abs1", [P, G, PACK], F32)
+        abs2 = tile("abs2", [P, PACK], F32)
+        warm = tile("warm", [P, 1], F32)
+
+        w1_bf = tile("w1_bf", [P, PACK, R, PACK], BF16)
+        w2_bf = tile("w2_bf", [P, PACK, R, PACK], BF16)
+        w3_bf = tile("w3_bf", [P, D, PACK], BF16)
+        w1_codes = tile("w1_codes", [P, D], I32)
+        w1_scales = tile("w1_scales", [P, D], U8)
+        w2_scales = tile("w2_scales", [P, D], U8)
+        w3_codes = tile("w3_codes", [P, D], I32)
+        w3_scales = tile("w3_scales", [P, D], U8)
+        w1_pad = tile("w1_pad", [P, LEAD + PACK * D + 1], I32)
+        w1_plane = tile("w1_plane", [P, PLANE], I32)
+        w2_stage = tile("w2_stage", [P, G, SLOT], I32)
+        w2_pad = tile("w2_pad", [P, LEAD + G * PACK * D + 1], I32)
+
+        state_bf = [tile("state_bf%d" % s, [P, N, PACK], BF16) for s in range(3)]
+        state_codes = [tile("state_codes%d" % s, [P, N], I32) for s in range(3)]
+        state_scales = [tile("state_scales%d" % s, [P, N], U8) for s in range(3)]
+        pre = [tile("pre%d" % s, [P, G, PACK, C], F32) for s in range(2)]
+        y = tile("y", [P, G, N], F32)
+
+        def rows(r):
+            return slice(R * r, R * r + R)
+
+        def cols(c, width=C):
+            return slice(width * c, width * c + width)
+
+        def by_head(t):
+            return t.rearrange("g (p j) n -> (g p) j n", j=PACK)
+
+        def quantize(codes, scales, values):
+            nc.vector.quantize_mx(out=codes.bitcast(FP8X4), scales=scales, in_=values)
+
+        def quantize_state(s, n0, n1):
+            quantize(state_codes[s][:, n0:n1], state_scales[s][:, n0:n1],
+                     state_bf[s][:, n0:n1, :].rearrange("p n j -> p (n j)"))
+
+        def double_scales(plane, scales):
+            both = plane[:, 16:80].rearrange("p (x c w) -> p x c w", c=2, w=8)
+            once = scales[:].bitcast(I32).rearrange("p (x w) -> p x w", w=8)
+            for c in range(2):
+                nc.vector.tensor_copy(out=both[:, :, c, :], in_=once)
+
+        def window(pad, plane, r, piece, x, place):
+            c0 = LEAD + D * piece - R * place
+            s0 = 64 + 64 * x - 64 * (place // 2)
+            return pad[rows(r), c0:c0 + D].bitcast(FP8X4), plane.bitcast(U8)[rows(r), s0:s0 + D]
+
+        def mx(dst, weights, weight_scales, s, r, c, start, stop):
+            nc.tensor.matmul_mx(out=dst, lhsT=weights, lhsT_scale=weight_scales,
+                                rhs=state_codes[s][rows(r), cols(c)].bitcast(FP8X4),
+                                rhs_scale=state_scales[s][rows(r), cols(c)], start=start, stop=stop)
+
+        def load_x1(queue, g):
+            src = x1[g].rearrange("(p x) n -> p x n", x=PACK)
+            for q in QUADRANT_ORDER:
+                queue.dma_start(out=x1_raw[rows(q), g, :, :], in_=src[:, :, cols(q)])
+
+        def cast_h(half):
+            n0 = 256 * half
+            view = h_raw[:].rearrange("p j n -> p n j")
+            nc.scalar.copy(out=state_bf[0][:, n0 + H_SPLIT:n0 + 256, :], in_=view[:, n0 + H_SPLIT:n0 + 256, :])
+            nc.vector.tensor_copy(out=state_bf[0][:, n0:n0 + H_SPLIT, :], in_=view[:, n0:n0 + H_SPLIT, :])
+            quantize_state(0, n0, n0 + 256)
+
+        def step1_passes(q):
+            for x in range(PACK):
+                for g in range(G):
+                    wt, ws = window(w1_pad, w1_plane[:], g, x, x, q)
+                    mx(bank_a[g][:, cols(x)], wt, ws, 0, g, q, q == 0 and x == 0, q == G - 1 and x == PACK - 1)
+
+        def step2_passes(g):
+            for x in range(PACK):
+                for r in range(G):
+                    s = SLOT_OF_SHIFT[(r - g) % G]
+                    wt, ws = window(w2_pad, w2_stage[:, s, D:], r, PACK * s + x, x, g)
+                    mx(bank_b[r][:, cols(x)], wt, ws, 1, r, g, g == HEAD_ORDER[0] and x == 0, g == HEAD_ORDER[-1] and x == PACK - 1)
+
+        def step3_passes(c):
+            for g in range(G):
+                bank = bank_a[g] if c < 2 else bank_b[g]
+                mx(bank[:, cols(c % 2)], w3_codes[rows(g), :].bitcast(FP8X4), w3_scales[rows(g), :], 2, g, c, True, True)
+
+        def scale_on_scalar(dst, factor):
+            nc.scalar.activation(out=dst, in_=dst, func=ACT.Copy, scale=factor)
+
+        def scale_on_gpsimd(dst, factor):
+            nc.gpsimd.tensor_scalar(out=dst, in0=dst, scalar1=factor, scalar2=0.0, op0=ALU.mult, op1=ALU.add)
+
+        def scale_on_vector(dst, factor):
+            nc.vector.tensor_scalar(out=dst, in0=dst, scalar1=factor, scalar2=None, op0=ALU.mult)
+
+        def add1(g):
+            for x in range(PACK):
+                nc.vector.scalar_tensor_tensor(out=pre[0][:, g, x, :], in0=bank_a[g][:, cols(x)], scalar=abs1[:, g, x:x + 1],
+                                               in1=x1_raw[:, g, x, :], op0=ALU.mult, op1=ALU.add)
+
+        def add2(r):
+            for x in range(PACK):
+                nc.vector.scalar_tensor_tensor(out=pre[1][:, r, x, :], in0=bank_b[r][:, cols(x)], scalar=abs2[:, x:x + 1],
+                                               in1=x2_raw[:, x, cols(r)], op0=ALU.mult, op1=ALU.add)
+
+        def relu(s, c):
+            nc.scalar.activation(out=state_bf[s + 1][:, cols(c), :], in_=pre[s][:, c, :, :].rearrange("p x n -> p n x"), func=ACT.Relu)
+
+        def finish(half, g):
+            bank = bank_a[g] if half == 0 else bank_b[g]
+            piece = y[:, g, cols(half, 256)]
+            nc.vector.tensor_tensor(out=piece, in0=bank[:, 0:256], in1=x3_raw[:, g, cols(half, 256)], op=ALU.add)
+            nc.scalar.activation(out=piece, in_=piece, func=ACT.Relu)
+            nc.sync.dma_start(out=out[g][:, cols(half, 256)], in_=piece)
+
+        nc.sync.dma_start(out=a1_head[:], in_=a1.rearrange("g (p j) o -> (g p) (j o)", j=PACK))
+        nc.sync.dma_start(out=w1_raw[:], in_=by_head(w1))
+        nc.sync.dma_start(out=w2_raw[:], in_=by_head(w2))
+        for half in range(2):
+            nc.sync.dma_start(out=h_raw[:, :, cols(half, 256)], in_=by_head(h)[:, :, cols(half, 256)])
+        load_x1(nc.sync, 0)
+        load_x1(nc.sync, 1)
+        for q in QUADRANT_ORDER:
+            nc.gpsimd.dma_start(out=a1_all[rows(q), :, :], in_=a1.rearrange("g (p j) o -> p g (j o)", j=PACK))
+        load_x1(nc.gpsimd, 3)
+        nc.gpsimd.dma_start(out=a2_head[:], in_=a2.rearrange("g (p j) o -> (g p) (j o)", j=PACK))
+
+        nc.vector.memset(warm[:], 0.0)
+        nc.scalar.activation(out=warm[:], in_=warm[:], func=ACT.Relu)
+        nc.vector.memset(w1_scales[:].bitcast(I32), 0)
+        nc.vector.memset(w2_scales[:].bitcast(I32), 0)
+        nc.vector.memset(w1_plane[:], 0)
+        nc.vector.memset(w2_stage[:, 0, D:], 0)
+        nc.vector.memset(w1_pad[:], 0)
+        nc.vector.memset(w2_pad[:], 0)
+
+        nc.scalar.copy(out=w1_bf[:], in_=w1_raw[:].rearrange("p j (m x) -> p x m j", x=PACK))
+        nc.scalar.activation(out=sign1[:], in_=a1_head[:], func=ACT.Sign)
+        quantize(w1_codes[:], w1_scales[:], w1_bf[:].rearrange("p x m j -> p (x m j)"))
+        nc.vector.tensor_tensor(out=w2_bf[:], in0=w2_raw[:].rearrange("p j (m x) -> p x m j", x=PACK),
+                                in1=sign1[:].unsqueeze(1).unsqueeze(1).to_broadcast([P, PACK, R, PACK]), op=ALU.mult)
+        nc.vector.tensor_copy(out=w1_pad[:, LEAD:LEAD + PACK * D].rearrange("p (x w) -> p x w", w=D)[:, :, 0:R],
+                              in_=w1_codes[:].rearrange("p (x w) -> p x w", w=R))
+        quantize(w2_stage[:, 0, 0:D], w2_scales[:], w2_bf[:].rearrange("p x m j -> p (x m j)"))
+        double_scales(w1_plane[:], w1_scales)
+        double_scales(w2_stage[:, 0, D:], w2_scales)
+        for p0 in (0, 64):
+            nc.sync.dma_start(out=w2_stage[64 - p0:128 - p0, 1, :], in_=w2_stage[p0:p0 + 64, 0, :])
+        load_x1(nc.sync, 2)
+        for p0, p1 in ((0, 64), (64, 96), (96, 128)):
+            d0 = (p0 + R) % P
+            nc.sync.dma_start(out=w2_stage[d0:d0 + p1 - p0, 2:4, :], in_=w2_stage[p0:p1, 0:2, :])
+        nc.sync.dma_start(out=w3_raw[:], in_=by_head(w3))
+        for half in range(2):
+            nc.sync.dma_start(out=x2_raw[:, :, cols(half, 256)], in_=by_head(x2)[:, :, cols(half, 256)])
+        nc.sync.dma_start(out=x3_raw[:], in_=x3.rearrange("g l n -> l g n"))
+
+        cast_h(0)
+        step1_passes(0)
+        step1_passes(1)
+        cast_h(1)
+        step1_passes(2)
+        step1_passes(3)
+        nc.scalar.activation(out=abs1[:], in_=a1_all[:], func=ACT.Abs)
+        for g, scale in ((0, scale_on_scalar), (3, scale_on_scalar), (1, scale_on_gpsimd)):
+            for x in range(PACK):
+                scale(x1_raw[:, g, x, :], abs1[:, g, x:x + 1])
+        for i, g in enumerate(HEAD_ORDER):
+            if i == 3:
+                for x in range(PACK):
+                    scale_on_vector(x1_raw[:, g, x, :], abs1[:, g, x:x + 1])
+                nc.vector.tensor_copy(out=w2_pad[:, LEAD:LEAD + G * PACK * D].rearrange("p (s x w) -> p s x w", x=PACK, w=D)[:, :, :, 0:R],
+                                      in_=w2_stage[:, :, 0:D].rearrange("p s (x w) -> p s x w", w=R))
+                step2_passes(HEAD_ORDER[0])
+                step2_passes(HEAD_ORDER[1])
+            add1(g)
+            relu(0, g)
+            if i == 2:
+                nc.scalar.activation(out=abs2[:], in_=a2_head[:], func=ACT.Abs)
+                nc.scalar.activation(out=sign2[:], in_=a2_head[:], func=ACT.Sign)
+            if i >= 1:
+                before = HEAD_ORDER[i - 1]
+                quantize_state(1, C * before, C * before + C)
+        step2_passes(HEAD_ORDER[2])
+        nc.vector.tensor_tensor(out=w3_bf[:], in0=w3_raw[:].rearrange("p j m -> p m j"),
+                                in1=sign2[:].unsqueeze(1).to_broadcast([P, D, PACK]), op=ALU.mult)
+        quantize_state(1, C * HEAD_ORDER[3], C * HEAD_ORDER[3] + C)
+        step2_passes(HEAD_ORDER[3])
+        quantize(w3_codes[:], w3_scales[:], w3_bf[:].rearrange("p m j -> p (m j)"))
+        for x in range(PACK):
+            scale_on_vector(x2_raw[:, x, 0:256], abs2[:, x:x + 1])
+            scale_on_scalar(x2_raw[:, x, 256:512], abs2[:, x:x + 1])
+
+        for r in range(G):
+            add2(r)
+            relu(1, r)
+            if r >= 1:
+                quantize_state(2, C * (r - 1), C * r)
+                step3_passes(r - 1)
+        finish(0, 0)
+        finish(0, 1)
+        quantize_state(2, C * 3, C * 4)
+        step3_passes(3)
+        finish(0, 2)
+        finish(0, 3)
+        for g in range(G):
+            finish(1, g)

@@ -17,11 +17,13 @@ P = 128
 R = 32
 PACK = 4
 C = 128
+HALF = 256
 LEAD = 96
 PLANE = 96
 SLOT = D + PLANE
 H_SPLIT = 176
-HEAD_ORDER = (0, 3, 1, 2)
+LAST_SPLIT = 80
+HEAD_ORDER = (0, 1, 2, 3)
 QUADRANT_ORDER = (0, 2, 1, 3)
 SLOT_OF_SHIFT = (0, 2, 1, 3)
 
@@ -42,9 +44,10 @@ def tile_rows_steps_relu_kernel(tc, h, w1, x1, a1, w2, x2, a2, w3, x3, out):
         w1_raw = tile("w1_raw", [P, PACK, D], F32)
         w2_raw = tile("w2_raw", [P, PACK, D], F32)
         w3_raw = tile("w3_raw", [P, PACK, D], F32)
-        h_raw = tile("h_raw", [P, PACK, N], F32)
+        h_pieces = ((0, C), (C, HALF), (HALF, N))
+        h_raw = [tile("h_raw%d" % i, [P, PACK, n1 - n0], F32) for i, (n0, n1) in enumerate(h_pieces)]
         x1_raw = tile("x1_raw", [P, G, PACK, C], F32)
-        x2_raw = tile("x2_raw", [P, PACK, N], F32)
+        x2_raw = tile("x2_raw", [P, 2, PACK, HALF], F32)
         x3_raw = tile("x3_raw", [P, G, N], F32)
         a1_head = tile("a1_head", [P, PACK], F32)
         a2_head = tile("a2_head", [P, PACK], F32)
@@ -58,21 +61,18 @@ def tile_rows_steps_relu_kernel(tc, h, w1, x1, a1, w2, x2, a2, w3, x3, out):
         w1_bf = tile("w1_bf", [P, PACK, R, PACK], BF16)
         w2_bf = tile("w2_bf", [P, PACK, R, PACK], BF16)
         w3_bf = tile("w3_bf", [P, D, PACK], BF16)
-        w1_codes = tile("w1_codes", [P, D], I32)
-        w1_scales = tile("w1_scales", [P, D], U8)
-        w2_scales = tile("w2_scales", [P, D], U8)
         w3_codes = tile("w3_codes", [P, D], I32)
         w3_scales = tile("w3_scales", [P, D], U8)
-        w1_pad = tile("w1_pad", [P, LEAD + PACK * D + 1], I32)
+        w1_pad = tile("w1_pad", [P, PACK + 1, D], I32)
         w1_plane = tile("w1_plane", [P, PLANE], I32)
         w2_stage = tile("w2_stage", [P, G, SLOT], I32)
-        w2_pad = tile("w2_pad", [P, LEAD + G * PACK * D + 1], I32)
+        w2_pad = tile("w2_pad", [P, G * PACK + 1, D], I32)
 
         state_bf = [tile("state_bf%d" % s, [P, N, PACK], BF16) for s in range(3)]
         state_codes = [tile("state_codes%d" % s, [P, N], I32) for s in range(3)]
         state_scales = [tile("state_scales%d" % s, [P, N], U8) for s in range(3)]
         pre = [tile("pre%d" % s, [P, G, PACK, C], F32) for s in range(2)]
-        y = tile("y", [P, G, N], F32)
+        y = tile("y", [P, 2, G, HALF], F32)
 
         def rows(r):
             return slice(R * r, R * r + R)
@@ -90,46 +90,55 @@ def tile_rows_steps_relu_kernel(tc, h, w1, x1, a1, w2, x2, a2, w3, x3, out):
             quantize(state_codes[s][:, n0:n1], state_scales[s][:, n0:n1],
                      state_bf[s][:, n0:n1, :].rearrange("p n j -> p (n j)"))
 
-        def double_scales(plane, scales):
+        def quantize_dealt(codes, first, step, plane, values):
+            for x in range(PACK):
+                c0 = first + step * x
+                quantize(codes[:, c0:c0 + R], plane.bitcast(U8)[:, 64 + 64 * x:96 + 64 * x],
+                         values[:, x, :, :].rearrange("p m j -> p (m j)"))
+
+        def double_scales(plane):
             both = plane[:, 16:80].rearrange("p (x c w) -> p x c w", c=2, w=8)
-            once = scales[:].bitcast(I32).rearrange("p (x w) -> p x w", w=8)
-            for c in range(2):
-                nc.vector.tensor_copy(out=both[:, :, c, :], in_=once)
+            nc.vector.tensor_copy(out=both[:, :, 1, :], in_=both[:, :, 0, :])
 
         def window(pad, plane, r, piece, x, place):
             c0 = LEAD + D * piece - R * place
             s0 = 64 + 64 * x - 64 * (place // 2)
-            return pad[rows(r), c0:c0 + D].bitcast(FP8X4), plane.bitcast(U8)[rows(r), s0:s0 + D]
+            return pad[:].rearrange("p i w -> p (i w)")[rows(r), c0:c0 + D].bitcast(FP8X4), plane.bitcast(U8)[rows(r), s0:s0 + D]
 
         def mx(dst, weights, weight_scales, s, r, c, start, stop):
             nc.tensor.matmul_mx(out=dst, lhsT=weights, lhsT_scale=weight_scales,
                                 rhs=state_codes[s][rows(r), cols(c)].bitcast(FP8X4),
                                 rhs_scale=state_scales[s][rows(r), cols(c)], start=start, stop=stop)
 
-        def load_x1(queue, g):
+        def load_h(i):
+            n0, n1 = h_pieces[i]
+            nc.sync.dma_start(out=h_raw[i][:], in_=by_head(h)[:, :, n0:n1])
+
+        def load_x1(queue, g, quadrants=QUADRANT_ORDER):
             src = x1[g].rearrange("(p x) n -> p x n", x=PACK)
-            for q in QUADRANT_ORDER:
+            for q in quadrants:
                 queue.dma_start(out=x1_raw[rows(q), g, :, :], in_=src[:, :, cols(q)])
 
-        def cast_h(half):
-            n0 = 256 * half
-            view = h_raw[:].rearrange("p j n -> p n j")
-            nc.scalar.copy(out=state_bf[0][:, n0 + H_SPLIT:n0 + 256, :], in_=view[:, n0 + H_SPLIT:n0 + 256, :])
-            nc.vector.tensor_copy(out=state_bf[0][:, n0:n0 + H_SPLIT, :], in_=view[:, n0:n0 + H_SPLIT, :])
-            quantize_state(0, n0, n0 + 256)
+        def cast_h(i, on_vector):
+            n0, n1 = h_pieces[i]
+            view = h_raw[i][:].rearrange("p j n -> p n j")
+            nc.scalar.copy(out=state_bf[0][:, n0 + on_vector:n1, :], in_=view[:, on_vector:, :])
+            if on_vector:
+                nc.vector.tensor_copy(out=state_bf[0][:, n0:n0 + on_vector, :], in_=view[:, :on_vector, :])
 
-        def step1_passes(q):
-            for x in range(PACK):
-                for g in range(G):
-                    wt, ws = window(w1_pad, w1_plane[:], g, x, x, q)
-                    mx(bank_a[g][:, cols(x)], wt, ws, 0, g, q, q == 0 and x == 0, q == G - 1 and x == PACK - 1)
+        def step1_pass(g, q, x):
+            wt, ws = window(w1_pad, w1_plane[:], g, x, x, q)
+            mx(bank_a[g][:, cols(x)], wt, ws, 0, g, q, q == 0 and x == 0, q == G - 1 and x == PACK - 1)
 
-        def step2_passes(g):
+        def step2_pass(r, g, x):
+            s = SLOT_OF_SHIFT[(r - g) % G]
+            wt, ws = window(w2_pad, w2_stage[:, s, D:], r, PACK * s + x, x, g)
+            mx(bank_b[r][:, cols(x)], wt, ws, 1, r, g, g == HEAD_ORDER[0] and x == 0, g == HEAD_ORDER[-1] and x == PACK - 1)
+
+        def step2_passes(g, tiles):
             for x in range(PACK):
-                for r in range(G):
-                    s = SLOT_OF_SHIFT[(r - g) % G]
-                    wt, ws = window(w2_pad, w2_stage[:, s, D:], r, PACK * s + x, x, g)
-                    mx(bank_b[r][:, cols(x)], wt, ws, 1, r, g, g == HEAD_ORDER[0] and x == 0, g == HEAD_ORDER[-1] and x == PACK - 1)
+                for r in tiles:
+                    step2_pass(r, g, x)
 
         def step3_passes(c):
             for g in range(G):
@@ -153,99 +162,119 @@ def tile_rows_steps_relu_kernel(tc, h, w1, x1, a1, w2, x2, a2, w3, x3, out):
         def add2(r):
             for x in range(PACK):
                 nc.vector.scalar_tensor_tensor(out=pre[1][:, r, x, :], in0=bank_b[r][:, cols(x)], scalar=abs2[:, x:x + 1],
-                                               in1=x2_raw[:, x, cols(r)], op0=ALU.mult, op1=ALU.add)
+                                               in1=x2_raw[:, r // 2, x, cols(r % 2)], op0=ALU.mult, op1=ALU.add)
 
-        def relu(s, c):
-            nc.scalar.activation(out=state_bf[s + 1][:, cols(c), :], in_=pre[s][:, c, :, :].rearrange("p x n -> p n x"), func=ACT.Relu)
+        def relu_on_scalar(s, c, first):
+            nc.scalar.activation(out=state_bf[s + 1][:, C * c + first:C * c + C, :],
+                                 in_=pre[s][:, c, :, first:].rearrange("p x n -> p n x"), func=ACT.Relu)
+
+        def relu_on_vector(s, c, count):
+            nc.vector.tensor_scalar(out=state_bf[s + 1][:, C * c:C * c + count, :], in0=pre[s][:, c, :, :count].rearrange("p x n -> p n x"),
+                                    scalar1=0.0, scalar2=None, op0=ALU.max)
 
         def finish(half, g):
             bank = bank_a[g] if half == 0 else bank_b[g]
-            piece = y[:, g, cols(half, 256)]
-            nc.vector.tensor_tensor(out=piece, in0=bank[:, 0:256], in1=x3_raw[:, g, cols(half, 256)], op=ALU.add)
+            piece = y[:, half, g, :]
+            nc.vector.tensor_tensor(out=piece, in0=bank[:, 0:HALF], in1=x3_raw[:, g, cols(half, HALF)], op=ALU.add)
             nc.scalar.activation(out=piece, in_=piece, func=ACT.Relu)
-            nc.sync.dma_start(out=out[g][:, cols(half, 256)], in_=piece)
+            nc.sync.dma_start(out=out[g][:, cols(half, HALF)], in_=piece)
+
+        first, second, third, last = HEAD_ORDER
 
         nc.sync.dma_start(out=a1_head[:], in_=a1.rearrange("g (p j) o -> (g p) (j o)", j=PACK))
         nc.sync.dma_start(out=w1_raw[:], in_=by_head(w1))
+        load_h(0)
         nc.sync.dma_start(out=w2_raw[:], in_=by_head(w2))
-        for half in range(2):
-            nc.sync.dma_start(out=h_raw[:, :, cols(half, 256)], in_=by_head(h)[:, :, cols(half, 256)])
-        load_x1(nc.sync, 0)
-        load_x1(nc.sync, 1)
+        load_h(1)
+        load_h(2)
+        load_x1(nc.sync, first)
         for q in QUADRANT_ORDER:
             nc.gpsimd.dma_start(out=a1_all[rows(q), :, :], in_=a1.rearrange("g (p j) o -> p g (j o)", j=PACK))
-        load_x1(nc.gpsimd, 3)
-        nc.gpsimd.dma_start(out=a2_head[:], in_=a2.rearrange("g (p j) o -> (g p) (j o)", j=PACK))
+        load_x1(nc.gpsimd, third)
 
         nc.vector.memset(warm[:], 0.0)
         nc.scalar.activation(out=warm[:], in_=warm[:], func=ACT.Relu)
-        nc.vector.memset(w1_scales[:].bitcast(I32), 0)
-        nc.vector.memset(w2_scales[:].bitcast(I32), 0)
         nc.vector.memset(w1_plane[:], 0)
         nc.vector.memset(w2_stage[:, 0, D:], 0)
-        nc.vector.memset(w1_pad[:], 0)
-        nc.vector.memset(w2_pad[:], 0)
+        nc.vector.memset(w1_pad[:, :, 0:LEAD], 0)
+        nc.vector.memset(w2_pad[:, :, 0:LEAD], 0)
 
-        nc.scalar.copy(out=w1_bf[:], in_=w1_raw[:].rearrange("p j (m x) -> p x m j", x=PACK))
+        nc.vector.tensor_copy(out=w1_bf[:], in_=w1_raw[:].rearrange("p j (m x) -> p x m j", x=PACK))
         nc.scalar.activation(out=sign1[:], in_=a1_head[:], func=ACT.Sign)
-        quantize(w1_codes[:], w1_scales[:], w1_bf[:].rearrange("p x m j -> p (x m j)"))
+        cast_h(0, 0)
+        quantize_dealt(w1_pad[:].rearrange("p i w -> p (i w)"), LEAD, D, w1_plane[:], w1_bf)
+        double_scales(w1_plane[:])
+        quantize_state(0, 0, C)
+        for x in range(PACK):
+            for g in range(G):
+                step1_pass(g, 0, x)
         nc.vector.tensor_tensor(out=w2_bf[:], in0=w2_raw[:].rearrange("p j (m x) -> p x m j", x=PACK),
                                 in1=sign1[:].unsqueeze(1).unsqueeze(1).to_broadcast([P, PACK, R, PACK]), op=ALU.mult)
-        nc.vector.tensor_copy(out=w1_pad[:, LEAD:LEAD + PACK * D].rearrange("p (x w) -> p x w", w=D)[:, :, 0:R],
-                              in_=w1_codes[:].rearrange("p (x w) -> p x w", w=R))
-        quantize(w2_stage[:, 0, 0:D], w2_scales[:], w2_bf[:].rearrange("p x m j -> p (x m j)"))
-        double_scales(w1_plane[:], w1_scales)
-        double_scales(w2_stage[:, 0, D:], w2_scales)
+        cast_h(1, 0)
+        quantize_dealt(w2_stage[:, 0, :], 0, R, w2_stage[:, 0, D:], w2_bf)
+        quantize_state(0, C, HALF)
+        for x in range(PACK):
+            for g in range(G):
+                step1_pass(g, 1, x)
+        double_scales(w2_stage[:, 0, D:])
         for p0 in (0, 64):
             nc.sync.dma_start(out=w2_stage[64 - p0:128 - p0, 1, :], in_=w2_stage[p0:p0 + 64, 0, :])
-        load_x1(nc.sync, 2)
+        load_x1(nc.sync, second)
+        load_x1(nc.sync, last, QUADRANT_ORDER[:2])
         for p0, p1 in ((0, 64), (64, 96), (96, 128)):
             d0 = (p0 + R) % P
             nc.sync.dma_start(out=w2_stage[d0:d0 + p1 - p0, 2:4, :], in_=w2_stage[p0:p1, 0:2, :])
+        load_x1(nc.sync, last, QUADRANT_ORDER[2:])
+        nc.sync.dma_start(out=a2_head[:], in_=a2.rearrange("g (p j) o -> (g p) (j o)", j=PACK))
+        nc.sync.dma_start(out=x2_raw[:, 0, :, :], in_=by_head(x2)[:, :, cols(0, HALF)])
         nc.sync.dma_start(out=w3_raw[:], in_=by_head(w3))
-        for half in range(2):
-            nc.sync.dma_start(out=x2_raw[:, :, cols(half, 256)], in_=by_head(x2)[:, :, cols(half, 256)])
+        nc.sync.dma_start(out=x2_raw[:, 1, :, :], in_=by_head(x2)[:, :, cols(1, HALF)])
         nc.sync.dma_start(out=x3_raw[:], in_=x3.rearrange("g l n -> l g n"))
 
-        cast_h(0)
-        step1_passes(0)
-        step1_passes(1)
-        cast_h(1)
-        step1_passes(2)
-        step1_passes(3)
+        cast_h(2, H_SPLIT)
         nc.scalar.activation(out=abs1[:], in_=a1_all[:], func=ACT.Abs)
-        for g, scale in ((0, scale_on_scalar), (3, scale_on_scalar), (1, scale_on_gpsimd)):
+        quantize_state(0, HALF, N)
+        left = {g: [(q, x) for q in (2, 3) for x in range(PACK)] for g in range(G)}
+        for g in [first, second, first, third, first, second, first, last] * 2 + [second, third, second, last] * 2 + [third, last] * 4:
+            step1_pass(g, *left[g].pop(0))
+        for g, scale in ((first, scale_on_scalar), (second, scale_on_scalar), (third, scale_on_gpsimd), (last, scale_on_gpsimd)):
             for x in range(PACK):
                 scale(x1_raw[:, g, x, :], abs1[:, g, x:x + 1])
-        for i, g in enumerate(HEAD_ORDER):
-            if i == 3:
-                for x in range(PACK):
-                    scale_on_vector(x1_raw[:, g, x, :], abs1[:, g, x:x + 1])
-                nc.vector.tensor_copy(out=w2_pad[:, LEAD:LEAD + G * PACK * D].rearrange("p (s x w) -> p s x w", x=PACK, w=D)[:, :, :, 0:R],
-                                      in_=w2_stage[:, :, 0:D].rearrange("p s (x w) -> p s x w", w=R))
-                step2_passes(HEAD_ORDER[0])
-                step2_passes(HEAD_ORDER[1])
-            add1(g)
-            relu(0, g)
-            if i == 2:
-                nc.scalar.activation(out=abs2[:], in_=a2_head[:], func=ACT.Abs)
-                nc.scalar.activation(out=sign2[:], in_=a2_head[:], func=ACT.Sign)
-            if i >= 1:
-                before = HEAD_ORDER[i - 1]
-                quantize_state(1, C * before, C * before + C)
-        step2_passes(HEAD_ORDER[2])
+        add1(first)
+        relu_on_scalar(0, first, 0)
+        add1(second)
+        relu_on_scalar(0, second, 0)
+        nc.vector.tensor_copy(out=w2_pad[:, 0:G * PACK, LEAD:].rearrange("p (s x) w -> p s x w", x=PACK),
+                              in_=w2_stage[:, :, 0:D].rearrange("p s (x w) -> p s x w", w=R))
+        quantize_state(1, C * first, C * first + C)
+        step2_passes(first, range(G))
+        add1(third)
+        relu_on_scalar(0, third, 0)
+        nc.scalar.activation(out=sign2[:], in_=a2_head[:], func=ACT.Sign)
+        nc.scalar.activation(out=abs2[:], in_=a2_head[:], func=ACT.Abs)
+        quantize_state(1, C * second, C * second + C)
+        step2_passes(second, range(G))
+        add1(last)
+        relu_on_scalar(0, last, LAST_SPLIT)
+        quantize_state(1, C * third, C * third + C)
+        relu_on_vector(0, last, LAST_SPLIT)
+        for x in range(2):
+            scale_on_vector(x2_raw[:, 0, x, :], abs2[:, x:x + 1])
+        quantize_state(1, C * last, C * last + C)
+        for tiles in ((0, 1), (2, 3)):
+            step2_passes(third, tiles)
+            step2_passes(last, tiles)
         nc.vector.tensor_tensor(out=w3_bf[:], in0=w3_raw[:].rearrange("p j m -> p m j"),
                                 in1=sign2[:].unsqueeze(1).to_broadcast([P, D, PACK]), op=ALU.mult)
-        quantize_state(1, C * HEAD_ORDER[3], C * HEAD_ORDER[3] + C)
-        step2_passes(HEAD_ORDER[3])
         quantize(w3_codes[:], w3_scales[:], w3_bf[:].rearrange("p m j -> p (m j)"))
+        for x in range(2, PACK):
+            scale_on_scalar(x2_raw[:, 0, x, :], abs2[:, x:x + 1])
         for x in range(PACK):
-            scale_on_vector(x2_raw[:, x, 0:256], abs2[:, x:x + 1])
-            scale_on_scalar(x2_raw[:, x, 256:512], abs2[:, x:x + 1])
+            scale_on_scalar(x2_raw[:, 1, x, :], abs2[:, x:x + 1])
 
         for r in range(G):
             add2(r)
-            relu(1, r)
+            relu_on_scalar(1, r, 0)
             if r >= 1:
                 quantize_state(2, C * (r - 1), C * r)
                 step3_passes(r - 1)

@@ -18,14 +18,9 @@ R = 32
 PACK = 4
 C = 128
 HALF = 256
-LEAD = 96
-PLANE = 96
-SLOT = D + PLANE
-H_SPLIT = 176
-LAST_SPLIT = 80
-HEAD_ORDER = (0, 1, 2, 3)
-QUADRANT_ORDER = (0, 2, 1, 3)
-SLOT_OF_SHIFT = (0, 2, 1, 3)
+H_ON_VECTOR = 176
+STATE_ON_VECTOR = 88
+HEAD_ORDER = (0, 2, 1, 3)
 
 
 def tile_rows_steps_relu_kernel(tc, h, w1, x1, a1, w2, x2, a2, w3, x3, out):
@@ -38,251 +33,168 @@ def tile_rows_steps_relu_kernel(tc, h, w1, x1, a1, w2, x2, a2, w3, x3, out):
         def tile(name, shape, dtype):
             return sb.tile(shape, dtype, name=name, align_bytes=64)
 
-        bank_a = [ps.tile([P, N], F32, name="bank_a%d" % r) for r in range(G)]
-        bank_b = [ps.tile([P, N], F32, name="bank_b%d" % r) for r in range(G)]
+        banks = [[ps.tile([P, N], F32, name="bank%d_%d" % (half, g)) for g in range(G)] for half in range(2)]
 
-        w1_raw = tile("w1_raw", [P, PACK, D], F32)
-        w2_raw = tile("w2_raw", [P, PACK, D], F32)
-        w3_raw = tile("w3_raw", [P, PACK, D], F32)
-        h_pieces = ((0, C), (C, HALF), (HALF, N))
-        h_raw = [tile("h_raw%d" % i, [P, PACK, n1 - n0], F32) for i, (n0, n1) in enumerate(h_pieces)]
-        x1_raw = tile("x1_raw", [P, G, PACK, C], F32)
-        x2_raw = tile("x2_raw", [P, 2, PACK, HALF], F32)
-        x3_raw = tile("x3_raw", [P, G, N], F32)
-        a1_head = tile("a1_head", [P, PACK], F32)
-        a2_head = tile("a2_head", [P, PACK], F32)
-        a1_all = tile("a1_all", [P, G, PACK], F32)
-        sign1 = tile("sign1", [P, PACK], F32)
-        sign2 = tile("sign2", [P, PACK], F32)
-        abs1 = tile("abs1", [P, G, PACK], F32)
-        abs2 = tile("abs2", [P, PACK], F32)
+        w_raw = [tile("w_raw%d" % s, [P, PACK, D], F32) for s in range(3)]
+        w_bf = [tile("w_bf%d" % s, [P, D, PACK], BF16) for s in range(3)]
+        w_codes = [tile("w_codes%d" % s, [P, D], I32) for s in range(3)]
+        w_scales = [tile("w_scales%d" % s, [P, D], U8) for s in range(3)]
+        h_raw = tile("h_raw", [P, 2, PACK, HALF], F32)
+        x_raw = [tile("x_raw%d" % s, [P, 2, G, HALF], F32) for s in range(3)]
+        a_head = [tile("a_head%d" % s, [P, PACK], F32) for s in range(2)]
+        a_rows = tile("a_rows", [P, R], F32)
+        a_cols = tile("a_cols", [P, R], F32)
+        a_abs = tile("a_abs", [P, R], F32)
+        a_sign = [tile("a_sign%d" % s, [P, PACK], F32) for s in range(2)]
         warm = tile("warm", [P, 1], F32)
-
-        w1_bf = tile("w1_bf", [P, PACK, R, PACK], BF16)
-        w2_bf = tile("w2_bf", [P, PACK, R, PACK], BF16)
-        w3_bf = tile("w3_bf", [P, D, PACK], BF16)
-        w3_codes = tile("w3_codes", [P, D], I32)
-        w3_scales = tile("w3_scales", [P, D], U8)
-        w1_pad = tile("w1_pad", [P, PACK + 1, D], I32)
-        w1_plane = tile("w1_plane", [P, PLANE], I32)
-        w2_stage = tile("w2_stage", [P, G, SLOT], I32)
-        w2_pad = tile("w2_pad", [P, G * PACK + 1, D], I32)
-
+        pre = [tile("pre%d" % s, [P, 2, G, HALF], BF16) for s in range(2)]
+        moved = [tile("moved%d" % s, [P, 2, PACK, HALF], BF16) for s in range(2)]
         state_bf = [tile("state_bf%d" % s, [P, N, PACK], BF16) for s in range(3)]
         state_codes = [tile("state_codes%d" % s, [P, N], I32) for s in range(3)]
         state_scales = [tile("state_scales%d" % s, [P, N], U8) for s in range(3)]
-        pre = [tile("pre%d" % s, [P, G, PACK, C], F32) for s in range(2)]
         y = tile("y", [P, 2, G, HALF], F32)
 
-        def rows(r):
-            return slice(R * r, R * r + R)
+        def rows(g):
+            return slice(R * g, R * g + R)
 
-        def cols(c, width=C):
+        def cols(c, width):
             return slice(width * c, width * c + width)
 
         def by_head(t):
             return t.rearrange("g (p j) n -> (g p) j n", j=PACK)
 
+        def factor(s, g):
+            return a_abs[:, 8 * g + 4 * s:8 * g + 4 * s + 1]
+
+        def load_x(s, half):
+            nc.sync.dma_start(out=x_raw[s][:, half, :, :], in_=(x1, x2, x3)[s].rearrange("g m n -> m g n")[:, :, cols(half, HALF)])
+
+        def load_h(half):
+            nc.sync.dma_start(out=h_raw[:, half, :, :], in_=by_head(h)[:, :, cols(half, HALF)])
+
+        def load_w(s):
+            nc.sync.dma_start(out=w_raw[s][:], in_=by_head((w1, w2, w3)[s]))
+
+        def load_a_head(s):
+            nc.sync.dma_start(out=a_head[s][:], in_=(a1, a2)[s].rearrange("g (p j) o -> (g p) (j o)", j=PACK))
+
+        def take_sign(s):
+            nc.scalar.activation(out=a_sign[s][:], in_=a_head[s][:], func=ACT.Sign)
+
         def quantize(codes, scales, values):
             nc.vector.quantize_mx(out=codes.bitcast(FP8X4), scales=scales, in_=values)
 
-        def quantize_state(s, n0, n1):
-            quantize(state_codes[s][:, n0:n1], state_scales[s][:, n0:n1],
-                     state_bf[s][:, n0:n1, :].rearrange("p n j -> p (n j)"))
+        def quantize_weights(s):
+            quantize(w_codes[s][:], w_scales[s][:], w_bf[s][:].rearrange("p m j -> p (m j)"))
 
-        def quantize_dealt(codes, first, step, plane, values):
-            for x in range(PACK):
-                c0 = first + step * x
-                quantize(codes[:, c0:c0 + R], plane.bitcast(U8)[:, 64 + 64 * x:96 + 64 * x],
-                         values[:, x, :, :].rearrange("p m j -> p (m j)"))
+        def cast_weights(s):
+            nc.vector.tensor_tensor(out=w_bf[s][:], in0=w_raw[s][:].rearrange("p j m -> p m j"),
+                                    in1=a_sign[s - 1][:].unsqueeze(1).to_broadcast([P, D, PACK]), op=ALU.mult)
 
-        def double_scales(plane):
-            both = plane[:, 16:80].rearrange("p (x c w) -> p x c w", c=2, w=8)
-            nc.vector.tensor_copy(out=both[:, :, 1, :], in_=both[:, :, 0, :])
+        def cast_h(half):
+            view = h_raw[:, half, :, :].rearrange("p j n -> p n j")
+            dst = state_bf[0][:, cols(half, HALF), :]
+            nc.scalar.copy(out=dst[:, H_ON_VECTOR:, :], in_=view[:, H_ON_VECTOR:, :])
+            nc.vector.tensor_copy(out=dst[:, :H_ON_VECTOR, :], in_=view[:, :H_ON_VECTOR, :])
 
-        def window(pad, plane, r, piece, x, place):
-            c0 = LEAD + D * piece - R * place
-            s0 = 64 + 64 * x - 64 * (place // 2)
-            return pad[:].rearrange("p i w -> p (i w)")[rows(r), c0:c0 + D].bitcast(FP8X4), plane.bitcast(U8)[rows(r), s0:s0 + D]
+        def relu_interleave(s, c):
+            view = moved[s][:, c // 2, :, cols(c % 2, C)].rearrange("p j n -> p n j")
+            dst = state_bf[s + 1][:, cols(c, C), :]
+            nc.scalar.activation(out=dst[:, STATE_ON_VECTOR:, :], in_=view[:, STATE_ON_VECTOR:, :], func=ACT.Relu)
+            nc.vector.tensor_scalar(out=dst[:, :STATE_ON_VECTOR, :], in0=view[:, :STATE_ON_VECTOR, :], scalar1=0.0, scalar2=None, op0=ALU.max)
 
-        def mx(dst, weights, weight_scales, s, r, c, start, stop):
-            nc.tensor.matmul_mx(out=dst, lhsT=weights, lhsT_scale=weight_scales,
-                                rhs=state_codes[s][rows(r), cols(c)].bitcast(FP8X4),
-                                rhs_scale=state_scales[s][rows(r), cols(c)], start=start, stop=stop)
+        def multiply(s, c0, c1):
+            n = slice(C * c0, C * c1)
+            quantize(state_codes[s][:, n], state_scales[s][:, n], state_bf[s][:, n, :].rearrange("p n j -> p (n j)"))
+            for c in range(c0, c1):
+                for g in HEAD_ORDER:
+                    nc.tensor.matmul_mx(out=banks[c // 2][g][:, cols(c % 2, C)], lhsT=w_codes[s][rows(g), :].bitcast(FP8X4),
+                                        lhsT_scale=w_scales[s][rows(g), :], rhs=state_codes[s][rows(g), cols(c, C)].bitcast(FP8X4),
+                                        rhs_scale=state_scales[s][rows(g), cols(c, C)], start=True, stop=True)
 
-        def load_h(i):
-            n0, n1 = h_pieces[i]
-            nc.sync.dma_start(out=h_raw[i][:], in_=by_head(h)[:, :, n0:n1])
+        def scale_x_on_scalar(s, half, heads):
+            for g in heads:
+                piece = x_raw[s][:, half, g, :]
+                nc.scalar.activation(out=piece, in_=piece, func=ACT.Copy, scale=factor(s, g))
 
-        def load_x1(queue, g, quadrants=QUADRANT_ORDER):
-            src = x1[g].rearrange("(p x) n -> p x n", x=PACK)
-            for q in quadrants:
-                queue.dma_start(out=x1_raw[rows(q), g, :, :], in_=src[:, :, cols(q)])
+        def scale_x_on_vector(s, half, heads):
+            for g in heads:
+                piece = x_raw[s][:, half, g, :]
+                nc.vector.tensor_scalar(out=piece, in0=piece, scalar1=factor(s, g), scalar2=None, op0=ALU.mult)
 
-        def cast_h(i, on_vector):
-            n0, n1 = h_pieces[i]
-            view = h_raw[i][:].rearrange("p j n -> p n j")
-            nc.scalar.copy(out=state_bf[0][:, n0 + on_vector:n1, :], in_=view[:, on_vector:, :])
-            if on_vector:
-                nc.vector.tensor_copy(out=state_bf[0][:, n0:n0 + on_vector, :], in_=view[:, :on_vector, :])
+        def add_and_move(s, half):
+            for g in HEAD_ORDER:
+                nc.vector.scalar_tensor_tensor(out=pre[s][:, half, g, :], in0=banks[half][g][:, 0:HALF], scalar=factor(s, g),
+                                               in1=x_raw[s][:, half, g, :], op0=ALU.mult, op1=ALU.add)
+                nc.sync.dma_start(out=moved[s][rows(g), half, :, :], in_=pre[s][:, half, g, :])
 
-        def step1_pass(g, q, x):
-            wt, ws = window(w1_pad, w1_plane[:], g, x, x, q)
-            mx(bank_a[g][:, cols(x)], wt, ws, 0, g, q, q == 0 and x == 0, q == G - 1 and x == PACK - 1)
-
-        def step2_pass(r, g, x):
-            s = SLOT_OF_SHIFT[(r - g) % G]
-            wt, ws = window(w2_pad, w2_stage[:, s, D:], r, PACK * s + x, x, g)
-            mx(bank_b[r][:, cols(x)], wt, ws, 1, r, g, g == HEAD_ORDER[0] and x == 0, g == HEAD_ORDER[-1] and x == PACK - 1)
-
-        def step2_passes(g, tiles):
-            for x in range(PACK):
-                for r in tiles:
-                    step2_pass(r, g, x)
-
-        def step3_passes(c):
-            for g in range(G):
-                bank = bank_a[g] if c < 2 else bank_b[g]
-                mx(bank[:, cols(c % 2)], w3_codes[rows(g), :].bitcast(FP8X4), w3_scales[rows(g), :], 2, g, c, True, True)
-
-        def scale_on_scalar(dst, factor):
-            nc.scalar.activation(out=dst, in_=dst, func=ACT.Copy, scale=factor)
-
-        def scale_on_gpsimd(dst, factor):
-            nc.gpsimd.tensor_scalar(out=dst, in0=dst, scalar1=factor, scalar2=0.0, op0=ALU.mult, op1=ALU.add)
-
-        def scale_on_vector(dst, factor):
-            nc.vector.tensor_scalar(out=dst, in0=dst, scalar1=factor, scalar2=None, op0=ALU.mult)
-
-        def add1(g):
-            for x in range(PACK):
-                nc.vector.scalar_tensor_tensor(out=pre[0][:, g, x, :], in0=bank_a[g][:, cols(x)], scalar=abs1[:, g, x:x + 1],
-                                               in1=x1_raw[:, g, x, :], op0=ALU.mult, op1=ALU.add)
-
-        def add2(r):
-            for x in range(PACK):
-                nc.vector.scalar_tensor_tensor(out=pre[1][:, r, x, :], in0=bank_b[r][:, cols(x)], scalar=abs2[:, x:x + 1],
-                                               in1=x2_raw[:, r // 2, x, cols(r % 2)], op0=ALU.mult, op1=ALU.add)
-
-        def relu_on_scalar(s, c, first):
-            nc.scalar.activation(out=state_bf[s + 1][:, C * c + first:C * c + C, :],
-                                 in_=pre[s][:, c, :, first:].rearrange("p x n -> p n x"), func=ACT.Relu)
-
-        def relu_on_vector(s, c, count):
-            nc.vector.tensor_scalar(out=state_bf[s + 1][:, C * c:C * c + count, :], in0=pre[s][:, c, :, :count].rearrange("p x n -> p n x"),
-                                    scalar1=0.0, scalar2=None, op0=ALU.max)
-
-        def finish(half, g):
-            bank = bank_a[g] if half == 0 else bank_b[g]
-            piece = y[:, half, g, :]
-            nc.vector.tensor_tensor(out=piece, in0=bank[:, 0:HALF], in1=x3_raw[:, g, cols(half, HALF)], op=ALU.add)
-            nc.scalar.activation(out=piece, in_=piece, func=ACT.Relu)
-            nc.sync.dma_start(out=out[g][:, cols(half, HALF)], in_=piece)
-
-        first, second, third, last = HEAD_ORDER
-
-        nc.sync.dma_start(out=a1_head[:], in_=a1.rearrange("g (p j) o -> (g p) (j o)", j=PACK))
-        nc.sync.dma_start(out=w1_raw[:], in_=by_head(w1))
-        load_h(0)
-        nc.sync.dma_start(out=w2_raw[:], in_=by_head(w2))
-        load_h(1)
-        load_h(2)
-        load_x1(nc.sync, first)
-        for q in QUADRANT_ORDER:
-            nc.gpsimd.dma_start(out=a1_all[rows(q), :, :], in_=a1.rearrange("g (p j) o -> p g (j o)", j=PACK))
-        load_x1(nc.gpsimd, third)
+        def finish(half):
+            for g in HEAD_ORDER:
+                piece = y[:, half, g, :]
+                nc.vector.tensor_tensor(out=piece, in0=banks[half][g][:, 0:HALF], in1=x_raw[2][:, half, g, :], op=ALU.add)
+                nc.scalar.activation(out=piece, in_=piece, func=ACT.Relu)
+                nc.sync.dma_start(out=out[g][:, cols(half, HALF)], in_=piece)
 
         nc.vector.memset(warm[:], 0.0)
         nc.scalar.activation(out=warm[:], in_=warm[:], func=ACT.Relu)
-        nc.vector.memset(w1_plane[:], 0)
-        nc.vector.memset(w2_stage[:, 0, D:], 0)
-        nc.vector.memset(w1_pad[:, :, 0:LEAD], 0)
-        nc.vector.memset(w2_pad[:, :, 0:LEAD], 0)
+        nc.vector.memset(a_rows[:], 0.0)
+        load_h(0)
+        load_w(0)
+        for s, a in enumerate((a1, a2)):
+            nc.sync.dma_start(out=a_rows[4 * s:P:8, :], in_=a.rearrange("g (b j) o -> b g (j o)", j=R))
+        load_h(1)
+        load_x(0, 0)
+        load_x(0, 1)
+        load_a_head(0)
+        load_w(1)
+        load_x(1, 0)
 
-        nc.vector.tensor_copy(out=w1_bf[:], in_=w1_raw[:].rearrange("p j (m x) -> p x m j", x=PACK))
-        nc.scalar.activation(out=sign1[:], in_=a1_head[:], func=ACT.Sign)
-        cast_h(0, 0)
-        quantize_dealt(w1_pad[:].rearrange("p i w -> p (i w)"), LEAD, D, w1_plane[:], w1_bf)
-        double_scales(w1_plane[:])
-        quantize_state(0, 0, C)
-        for x in range(PACK):
-            for g in range(G):
-                step1_pass(g, 0, x)
-        nc.vector.tensor_tensor(out=w2_bf[:], in0=w2_raw[:].rearrange("p j (m x) -> p x m j", x=PACK),
-                                in1=sign1[:].unsqueeze(1).unsqueeze(1).to_broadcast([P, PACK, R, PACK]), op=ALU.mult)
-        cast_h(1, 0)
-        quantize_dealt(w2_stage[:, 0, :], 0, R, w2_stage[:, 0, D:], w2_bf)
-        quantize_state(0, C, HALF)
-        for x in range(PACK):
-            for g in range(G):
-                step1_pass(g, 1, x)
-        double_scales(w2_stage[:, 0, D:])
-        for p0 in (0, 64):
-            nc.sync.dma_start(out=w2_stage[64 - p0:128 - p0, 1, :], in_=w2_stage[p0:p0 + 64, 0, :])
-        load_x1(nc.sync, second)
-        load_x1(nc.sync, last, QUADRANT_ORDER[:2])
-        for p0, p1 in ((0, 64), (64, 96), (96, 128)):
-            d0 = (p0 + R) % P
-            nc.sync.dma_start(out=w2_stage[d0:d0 + p1 - p0, 2:4, :], in_=w2_stage[p0:p1, 0:2, :])
-        load_x1(nc.sync, last, QUADRANT_ORDER[2:])
-        nc.sync.dma_start(out=a2_head[:], in_=a2.rearrange("g (p j) o -> (g p) (j o)", j=PACK))
-        nc.sync.dma_start(out=x2_raw[:, 0, :, :], in_=by_head(x2)[:, :, cols(0, HALF)])
-        nc.sync.dma_start(out=w3_raw[:], in_=by_head(w3))
-        nc.sync.dma_start(out=x2_raw[:, 1, :, :], in_=by_head(x2)[:, :, cols(1, HALF)])
-        nc.sync.dma_start(out=x3_raw[:], in_=x3.rearrange("g l n -> l g n"))
+        cast_h(0)
+        nc.vector.tensor_copy(out=w_bf[0][:], in_=w_raw[0][:].rearrange("p j m -> p m j"))
+        nc.vector.transpose(a_cols[:], a_rows[:])
+        nc.scalar.activation(out=a_abs[:], in_=a_cols[:], func=ACT.Abs)
+        quantize_weights(0)
+        multiply(0, 0, 2)
+        cast_h(1)
+        multiply(0, 2, 4)
+        scale_x_on_vector(0, 0, HEAD_ORDER[:2])
+        scale_x_on_scalar(0, 0, HEAD_ORDER[2:])
+        scale_x_on_scalar(0, 1, HEAD_ORDER)
+        take_sign(0)
+        add_and_move(0, 0)
+        add_and_move(0, 1)
+        load_x(1, 1)
+        load_w(2)
+        load_a_head(1)
+        load_x(2, 0)
 
-        cast_h(2, H_SPLIT)
-        nc.scalar.activation(out=abs1[:], in_=a1_all[:], func=ACT.Abs)
-        quantize_state(0, HALF, N)
-        left = {g: [(q, x) for q in (2, 3) for x in range(PACK)] for g in range(G)}
-        for g in [first, second, first, third, first, second, first, last] * 2 + [second, third, second, last] * 2 + [third, last] * 4:
-            step1_pass(g, *left[g].pop(0))
-        for g, scale in ((first, scale_on_scalar), (second, scale_on_scalar), (third, scale_on_gpsimd), (last, scale_on_gpsimd)):
-            for x in range(PACK):
-                scale(x1_raw[:, g, x, :], abs1[:, g, x:x + 1])
-        add1(first)
-        relu_on_scalar(0, first, 0)
-        add1(second)
-        relu_on_scalar(0, second, 0)
-        nc.vector.tensor_copy(out=w2_pad[:, 0:G * PACK, LEAD:].rearrange("p (s x) w -> p s x w", x=PACK),
-                              in_=w2_stage[:, :, 0:D].rearrange("p s (x w) -> p s x w", w=R))
-        quantize_state(1, C * first, C * first + C)
-        step2_passes(first, range(G))
-        add1(third)
-        relu_on_scalar(0, third, 0)
-        nc.scalar.activation(out=sign2[:], in_=a2_head[:], func=ACT.Sign)
-        nc.scalar.activation(out=abs2[:], in_=a2_head[:], func=ACT.Abs)
-        quantize_state(1, C * second, C * second + C)
-        step2_passes(second, range(G))
-        add1(last)
-        relu_on_scalar(0, last, LAST_SPLIT)
-        quantize_state(1, C * third, C * third + C)
-        relu_on_vector(0, last, LAST_SPLIT)
-        for x in range(2):
-            scale_on_vector(x2_raw[:, 0, x, :], abs2[:, x:x + 1])
-        quantize_state(1, C * last, C * last + C)
-        for tiles in ((0, 1), (2, 3)):
-            step2_passes(third, tiles)
-            step2_passes(last, tiles)
-        nc.vector.tensor_tensor(out=w3_bf[:], in0=w3_raw[:].rearrange("p j m -> p m j"),
-                                in1=sign2[:].unsqueeze(1).to_broadcast([P, D, PACK]), op=ALU.mult)
-        quantize(w3_codes[:], w3_scales[:], w3_bf[:].rearrange("p m j -> p (m j)"))
-        for x in range(2, PACK):
-            scale_on_scalar(x2_raw[:, 0, x, :], abs2[:, x:x + 1])
-        for x in range(PACK):
-            scale_on_scalar(x2_raw[:, 1, x, :], abs2[:, x:x + 1])
+        scale_x_on_scalar(1, 0, HEAD_ORDER[:2])
+        cast_weights(1)
+        relu_interleave(0, 0)
+        quantize_weights(1)
+        relu_interleave(0, 1)
+        multiply(1, 0, 1)
+        multiply(1, 1, 2)
+        scale_x_on_scalar(1, 0, HEAD_ORDER[2:])
+        relu_interleave(0, 2)
+        relu_interleave(0, 3)
+        multiply(1, 2, 3)
+        multiply(1, 3, 4)
+        scale_x_on_scalar(1, 1, HEAD_ORDER)
+        take_sign(1)
+        add_and_move(1, 0)
+        add_and_move(1, 1)
+        load_x(2, 1)
 
-        for r in range(G):
-            add2(r)
-            relu_on_scalar(1, r, 0)
-            if r >= 1:
-                quantize_state(2, C * (r - 1), C * r)
-                step3_passes(r - 1)
-        finish(0, 0)
-        finish(0, 1)
-        quantize_state(2, C * 3, C * 4)
-        step3_passes(3)
-        finish(0, 2)
-        finish(0, 3)
-        for g in range(G):
-            finish(1, g)
+        cast_weights(2)
+        relu_interleave(1, 0)
+        quantize_weights(2)
+        relu_interleave(1, 1)
+        multiply(2, 0, 1)
+        multiply(2, 1, 2)
+        relu_interleave(1, 2)
+        relu_interleave(1, 3)
+        multiply(2, 2, 3)
+        multiply(2, 3, 4)
+        finish(0)
+        finish(1)

from contextlib import ExitStack

import concourse.mybir as mybir

G, D, N = 4, 128, 512
FLOPS = 3 * 2 * G * D * D * N

F32 = mybir.dt.float32
BF16 = mybir.dt.bfloat16
I32 = mybir.dt.int32
U8 = mybir.dt.uint8
FP8X4 = mybir.dt.float8_e4m3fn_x4
ALU = mybir.AluOpType
ACT = mybir.ActivationFunctionType

P = 128
R = 32
PACK = 4
C = 128
HALF = 256
H_ON_VECTOR = 176
STATE_ON_VECTOR = 88
HEAD_ORDER = (0, 2, 1, 3)


def tile_rows_steps_relu_kernel(tc, h, w1, x1, a1, w2, x2, a2, w3, x3, out):
    nc = tc.nc
    with ExitStack() as ctx:
        sb = ctx.enter_context(tc.tile_pool(name="sb", bufs=1))
        ps = ctx.enter_context(tc.psum_pool(name="ps", bufs=1))
        ctx.enter_context(tc.manual_schedule())

        def tile(name, shape, dtype):
            return sb.tile(shape, dtype, name=name, align_bytes=64)

        banks = [[ps.tile([P, N], F32, name="bank%d_%d" % (half, g)) for g in range(G)] for half in range(2)]

        w_raw = [tile("w_raw%d" % s, [P, PACK, D], F32) for s in range(3)]
        w_bf = [tile("w_bf%d" % s, [P, D, PACK], BF16) for s in range(3)]
        w_codes = [tile("w_codes%d" % s, [P, D], I32) for s in range(3)]
        w_scales = [tile("w_scales%d" % s, [P, D], U8) for s in range(3)]
        h_raw = tile("h_raw", [P, 2, PACK, HALF], F32)
        x_raw = [tile("x_raw%d" % s, [P, 2, G, HALF], F32) for s in range(3)]
        a_head = [tile("a_head%d" % s, [P, PACK], F32) for s in range(2)]
        a_rows = tile("a_rows", [P, R], F32)
        a_cols = tile("a_cols", [P, R], F32)
        a_abs = tile("a_abs", [P, R], F32)
        a_sign = [tile("a_sign%d" % s, [P, PACK], F32) for s in range(2)]
        warm = tile("warm", [P, 1], F32)
        pre = [tile("pre%d" % s, [P, 2, G, HALF], BF16) for s in range(2)]
        moved = [tile("moved%d" % s, [P, 2, PACK, HALF], BF16) for s in range(2)]
        state_bf = [tile("state_bf%d" % s, [P, N, PACK], BF16) for s in range(3)]
        state_codes = [tile("state_codes%d" % s, [P, N], I32) for s in range(3)]
        state_scales = [tile("state_scales%d" % s, [P, N], U8) for s in range(3)]
        y = tile("y", [P, 2, G, HALF], F32)

        def rows(g):
            return slice(R * g, R * g + R)

        def cols(c, width):
            return slice(width * c, width * c + width)

        def by_head(t):
            return t.rearrange("g (p j) n -> (g p) j n", j=PACK)

        def factor(s, g):
            return a_abs[:, 8 * g + 4 * s:8 * g + 4 * s + 1]

        def load_x(s, half):
            nc.sync.dma_start(out=x_raw[s][:, half, :, :], in_=(x1, x2, x3)[s].rearrange("g m n -> m g n")[:, :, cols(half, HALF)])

        def load_h(half):
            nc.sync.dma_start(out=h_raw[:, half, :, :], in_=by_head(h)[:, :, cols(half, HALF)])

        def load_w(s):
            nc.sync.dma_start(out=w_raw[s][:], in_=by_head((w1, w2, w3)[s]))

        def load_a_head(s):
            nc.sync.dma_start(out=a_head[s][:], in_=(a1, a2)[s].rearrange("g (p j) o -> (g p) (j o)", j=PACK))

        def take_sign(s):
            nc.scalar.activation(out=a_sign[s][:], in_=a_head[s][:], func=ACT.Sign)

        def quantize(codes, scales, values):
            nc.vector.quantize_mx(out=codes.bitcast(FP8X4), scales=scales, in_=values)

        def quantize_weights(s):
            quantize(w_codes[s][:], w_scales[s][:], w_bf[s][:].rearrange("p m j -> p (m j)"))

        def cast_weights(s):
            nc.vector.tensor_tensor(out=w_bf[s][:], in0=w_raw[s][:].rearrange("p j m -> p m j"),
                                    in1=a_sign[s - 1][:].unsqueeze(1).to_broadcast([P, D, PACK]), op=ALU.mult)

        def cast_h(half):
            view = h_raw[:, half, :, :].rearrange("p j n -> p n j")
            dst = state_bf[0][:, cols(half, HALF), :]
            nc.scalar.copy(out=dst[:, H_ON_VECTOR:, :], in_=view[:, H_ON_VECTOR:, :])
            nc.vector.tensor_copy(out=dst[:, :H_ON_VECTOR, :], in_=view[:, :H_ON_VECTOR, :])

        def relu_interleave(s, c):
            view = moved[s][:, c // 2, :, cols(c % 2, C)].rearrange("p j n -> p n j")
            dst = state_bf[s + 1][:, cols(c, C), :]
            nc.scalar.activation(out=dst[:, STATE_ON_VECTOR:, :], in_=view[:, STATE_ON_VECTOR:, :], func=ACT.Relu)
            nc.vector.tensor_scalar(out=dst[:, :STATE_ON_VECTOR, :], in0=view[:, :STATE_ON_VECTOR, :], scalar1=0.0, scalar2=None, op0=ALU.max)

        def multiply(s, c0, c1):
            n = slice(C * c0, C * c1)
            quantize(state_codes[s][:, n], state_scales[s][:, n], state_bf[s][:, n, :].rearrange("p n j -> p (n j)"))
            for c in range(c0, c1):
                for g in HEAD_ORDER:
                    nc.tensor.matmul_mx(out=banks[c // 2][g][:, cols(c % 2, C)], lhsT=w_codes[s][rows(g), :].bitcast(FP8X4),
                                        lhsT_scale=w_scales[s][rows(g), :], rhs=state_codes[s][rows(g), cols(c, C)].bitcast(FP8X4),
                                        rhs_scale=state_scales[s][rows(g), cols(c, C)], start=True, stop=True)

        def scale_x_on_scalar(s, half, heads):
            for g in heads:
                piece = x_raw[s][:, half, g, :]
                nc.scalar.activation(out=piece, in_=piece, func=ACT.Copy, scale=factor(s, g))

        def scale_x_on_vector(s, half, heads):
            for g in heads:
                piece = x_raw[s][:, half, g, :]
                nc.vector.tensor_scalar(out=piece, in0=piece, scalar1=factor(s, g), scalar2=None, op0=ALU.mult)

        def add_and_move(s, half):
            for g in HEAD_ORDER:
                nc.vector.scalar_tensor_tensor(out=pre[s][:, half, g, :], in0=banks[half][g][:, 0:HALF], scalar=factor(s, g),
                                               in1=x_raw[s][:, half, g, :], op0=ALU.mult, op1=ALU.add)
                nc.sync.dma_start(out=moved[s][rows(g), half, :, :], in_=pre[s][:, half, g, :])

        def finish(half):
            for g in HEAD_ORDER:
                piece = y[:, half, g, :]
                nc.vector.tensor_tensor(out=piece, in0=banks[half][g][:, 0:HALF], in1=x_raw[2][:, half, g, :], op=ALU.add)
                nc.scalar.activation(out=piece, in_=piece, func=ACT.Relu)
                nc.sync.dma_start(out=out[g][:, cols(half, HALF)], in_=piece)

        nc.vector.memset(warm[:], 0.0)
        nc.scalar.activation(out=warm[:], in_=warm[:], func=ACT.Relu)
        nc.vector.memset(a_rows[:], 0.0)
        load_h(0)
        load_w(0)
        for s, a in enumerate((a1, a2)):
            nc.sync.dma_start(out=a_rows[4 * s:P:8, :], in_=a.rearrange("g (b j) o -> b g (j o)", j=R))
        load_h(1)
        load_x(0, 0)
        load_x(0, 1)
        load_a_head(0)
        load_w(1)
        load_x(1, 0)

        cast_h(0)
        nc.vector.tensor_copy(out=w_bf[0][:], in_=w_raw[0][:].rearrange("p j m -> p m j"))
        nc.vector.transpose(a_cols[:], a_rows[:])
        nc.scalar.activation(out=a_abs[:], in_=a_cols[:], func=ACT.Abs)
        quantize_weights(0)
        multiply(0, 0, 2)
        cast_h(1)
        multiply(0, 2, 4)
        scale_x_on_vector(0, 0, HEAD_ORDER[:2])
        scale_x_on_scalar(0, 0, HEAD_ORDER[2:])
        scale_x_on_scalar(0, 1, HEAD_ORDER)
        take_sign(0)
        add_and_move(0, 0)
        add_and_move(0, 1)
        load_x(1, 1)
        load_w(2)
        load_a_head(1)
        load_x(2, 0)

        scale_x_on_scalar(1, 0, HEAD_ORDER[:2])
        cast_weights(1)
        relu_interleave(0, 0)
        quantize_weights(1)
        relu_interleave(0, 1)
        multiply(1, 0, 1)
        multiply(1, 1, 2)
        scale_x_on_scalar(1, 0, HEAD_ORDER[2:])
        relu_interleave(0, 2)
        relu_interleave(0, 3)
        multiply(1, 2, 3)
        multiply(1, 3, 4)
        scale_x_on_scalar(1, 1, HEAD_ORDER)
        take_sign(1)
        add_and_move(1, 0)
        add_and_move(1, 1)
        load_x(2, 1)

        cast_weights(2)
        relu_interleave(1, 0)
        quantize_weights(2)
        relu_interleave(1, 1)
        multiply(2, 0, 1)
        multiply(2, 1, 2)
        relu_interleave(1, 2)
        relu_interleave(1, 3)
        multiply(2, 2, 3)
        multiply(2, 3, 4)
        finish(0)
        finish(1)
